import numpy as np
import ml_dtypes


def mxq(x, axis, fmt="e4m3"):
    dtype, down = {"e4m3": (ml_dtypes.float8_e4m3fn, 7), "e5m2": (ml_dtypes.float8_e5m2, 14)}[fmt]
    v = np.moveaxis(np.asarray(x, np.float32).astype(ml_dtypes.bfloat16).astype(np.float64), axis, -1)
    blocks = v.reshape(v.shape[:-1] + (-1, 32))
    amax = np.abs(blocks).max(-1, keepdims=True)
    byte = np.maximum(np.where(amax > 0, np.frexp(amax)[1] - 1 + 127, 0) - down, 1)
    scale = np.exp2(byte - 127.0)
    codes = (blocks / scale).astype(np.float32).astype(dtype).astype(np.float64)
    return np.moveaxis((codes * scale).reshape(v.shape), -1, axis)


WIDE = False


def mx_kscale(k):
    if not WIDE:
        return np.ones(k)
    levels = np.array([10, -10, 5, -5, 0])
    if k % 512:
        return np.exp2(np.random.permutation(np.resize(levels, k // 32))).repeat(32)
    a = np.empty((k // 512, 16))
    for p in range(k // 512):
        a[p, :8] = np.random.permutation(np.resize(levels, 8))
        for g in range(8):
            far = levels[np.abs(levels - a[p, g]) >= 10]
            a[p, g + 8] = far[np.random.randint(len(far))]
    return np.exp2(a.ravel()).repeat(32)


def f64(x):
    return np.asarray(x).astype(np.float64)


def striped(idx):
    return np.tile(idx.reshape(-1, 16).T, (8, 1)).astype(np.uint16)


def unstriped(offs):
    return offs[:16].T.reshape(-1).astype(np.int64)


def pack_weight(w):
    k, n = w.shape
    w = f64(np.asarray(w, np.float32).astype(ml_dtypes.bfloat16)).reshape(k // 32, 32, n)
    amax = np.abs(w).max(1)
    byte = np.clip(np.where(amax > 0, np.frexp(amax)[1] - 1 + 127 - 7, 1), 1, 254)
    scaled = (w * np.exp2(127.0 - byte)[:, None, :]).reshape(k, n).astype(np.float32)
    words = np.ascontiguousarray(scaled.reshape(k // 512, 128, 4, n).transpose(0, 1, 3, 2)).astype(ml_dtypes.float8_e4m3fn).view(np.uint8)
    return words, np.ascontiguousarray(byte.astype(np.uint8).reshape(k // 512, 16, n))


def unpack_weight(words, scales):
    g, p, n, _ = words.shape
    vals = np.ascontiguousarray(words).view(ml_dtypes.float8_e4m3fn).astype(np.float64) * np.repeat(np.exp2(scales.astype(np.float64) - 127.0), 8, axis=1)[..., None]
    return vals.transpose(0, 1, 3, 2).reshape(g * 512, n)


K, T, S, D, N, H, U = 1024, 4096, 1024, 4, 128, 512, 512


def setup_inputs():
    n = np.random.standard_normal
    s = mx_kscale(K)[:, None]
    u = mx_kscale(H)
    packed_xT = pack_weight(n((K, T)) * s)
    return {
        "x_words": packed_xT[0],
        "x_scales": packed_xT[1],
        "w1": (n((K, H)) / np.sqrt(K) / s).astype(np.float32),
        "flr": (np.random.uniform(-0.6, 0.3, (H, U))).astype(np.float32),
        "unit": (np.random.uniform(0.6, 1.4, (H, 1)) * u[:, None]).astype(np.float32),
        "w2": (n((H, N)) / np.sqrt(H) / u[:, None]).astype(np.float32),
        "offs": striped(np.random.permutation(T)[:S]),
        "got": striped(np.random.permutation(S)[:U]),
    }


def reference(x_words, x_scales, w1, flr, unit, w2, offs, got):
    xq = unpack_weight(x_words, x_scales)[:, unstriped(offs)]
    y = mxq(f64(w1), 0, "e4m3").T @ xq
    sg = y[:, unstriped(got)]
    sc = np.maximum(sg, f64(flr))
    sum4 = sc.reshape(len(sc), -1, D).sum(axis=2)
    dv = sc - (0.25 * np.repeat(sum4, D, axis=1))
    we = np.exp(1.2 * np.tanh(dv))
    hid = f64(unit) * (we * sc)
    return mxq(f64(w2), 0, "e4m3").T @ mxq(hid, 0, "e4m3")

@@ -1,0 +1,241 @@
+from contextlib import ExitStack
+
+import concourse.mybir as mybir
+
+K, T, S, D, N, H, U = 1024, 4096, 1024, 4, 128, 512, 512
+FLOPS = 2 * K * H * S + 2 * H * N * U
+
+F32 = mybir.dt.float32
+BF16 = mybir.dt.bfloat16
+I32 = mybir.dt.int32
+U32 = mybir.dt.uint32
+U16 = mybir.dt.uint16
+U8 = mybir.dt.uint8
+FP8X4 = mybir.dt.float8_e4m3fn_x4
+ALU = mybir.AluOpType
+ACT = mybir.ActivationFunctionType
+AX = mybir.AxisListType
+
+P = 128
+PACK = 4
+BANK = 512
+HALF = U // 2
+
+
+def tile_picked_yxtrim_soft_p_kernel(tc, x_words, x_scales, w1, flr, unit, w2, offs, got, out):
+    nc = tc.nc
+    with ExitStack() as ctx:
+        keep = ctx.enter_context(tc.tile_pool(name="keep", bufs=1))
+        psum = ctx.enter_context(tc.psum_pool(name="psum", bufs=1))
+
+        def sb(shape, dtype, name):
+            return keep.tile(shape, dtype, name=name, align_bytes=64)
+
+        offs_t = keep.tile([P, S // 16], U16, name="offs_t")
+        got_t = keep.tile([P, U // 16], U16, name="got_t")
+        xw = [sb([P, T], U32, "xw%d" % o) for o in range(2)]
+        xs = sb([P, T], U8, "xs")
+        w1a = sb([P, PACK, H], F32, "w1a")
+        w1b = [sb([P, PACK, H // 2], F32, "w1b%d" % c) for c in range(2)]
+        w2r = sb([P, PACK, N], F32, "w2r")
+        fl = [sb([P, 2, U], F32, "fl%d" % c) for c in range(2)]
+        un = sb([P, PACK], F32, "un")
+
+        def load_words(o):
+            nc.sync.dma_start(out=xw[o][:].bitcast(I32), in_=x_words[o].rearrange("p n t -> p (n t)").bitcast(I32))
+
+        nc.vector.memset(xs[:].bitcast(I32), 0)
+        load_words(0)
+        nc.sync.dma_start(offs_t[:], offs)
+        for q in range(4):
+            nc.gpsimd.dma_start(out=xs[32 * q : 32 * q + 8, :].bitcast(I32), in_=x_scales[:, 4 * q : 4 * q + 4, :].bitcast(I32))
+        w1v = w1.rearrange("(o p j) c -> o p j c", o=2, j=PACK)
+        nc.sync.dma_start(out=w1a[:], in_=w1v[0])
+        load_words(1)
+        for c in range(2):
+            nc.sync.dma_start(out=w1b[c][:], in_=w1v[1][:, :, c * 256 : (c + 1) * 256])
+        nc.sync.dma_start(out=w2r[:], in_=w2.rearrange("(p t) m -> p t m", t=PACK))
+        nc.sync.dma_start(got_t[:], got)
+        flv = flr.rearrange("(p t) r -> p t r", t=PACK)
+        nc.sync.dma_start(out=fl[0][:], in_=flv[:, 0:2, :])
+        nc.sync.dma_start(out=un[:], in_=unit.rearrange("(p t) one -> p (t one)", t=PACK))
+        nc.sync.dma_start(out=fl[1][:], in_=flv[:, 2:4, :])
+
+        gw = [sb([P, S], U32, "gw%d" % o) for o in range(2)]
+        gs = sb([P, S], U8, "gs")
+        wb = [sb([P, PACK * P * PACK], BF16, "wb%d" % o) for o in range(2)]
+        wc = [sb([P, H], U32, "wc%d" % o) for o in range(2)]
+        ws = [sb([P, H], U8, "ws%d" % o) for o in range(2)]
+
+        def deal(engine, o, raw, m0, m1, base):
+            dst = wb[o][:].rearrange("p (t m j) -> p m j t", t=PACK, j=PACK)[:, m0:m1]
+            src = raw[:].rearrange("p j (m t) -> p m j t", t=PACK)[:, m0 - base : m1 - base]
+            if engine == "scalar":
+                nc.scalar.activation(out=dst, in_=src, func=ACT.Copy)
+            else:
+                nc.vector.tensor_copy(out=dst, in_=src)
+
+        def quant_w1(o, t0, t1):
+            nc.vector.quantize_mx(out=wc[o][:, t0 * P : t1 * P].bitcast(FP8X4), scales=ws[o][:, t0 * P : t1 * P], in_=wb[o][:, t0 * 512 : t1 * 512])
+
+        banks = [[psum.tile([P, BANK], F32, name="bank%d%d" % (t, h), tag="bank%d%d" % (t, h)) for h in range(2)] for t in range(PACK)]
+
+        def product(o, t, h):
+            cols = slice(h * BANK, (h + 1) * BANK)
+            nc.tensor.matmul_mx(
+                out=banks[t][h][:],
+                lhsT=wc[o][:, t * P : (t + 1) * P].bitcast(FP8X4),
+                lhsT_scale=ws[o][:, t * P : (t + 1) * P],
+                rhs=gw[o][:, cols].bitcast(FP8X4),
+                rhs_scale=gs[4 * o : P, cols],
+                start=(o == 0),
+                stop=(o == 1),
+            )
+
+        nc.vector.tensor_copy(gw[0][:], xw[0][:].indirect(offs_t[:]))
+        nc.vector.tensor_copy(gs[:], xs[:].indirect(offs_t[:]))
+        deal("scalar", 0, w1a, 0, 128, 0)
+        quant_w1(0, 0, 4)
+        nc.vector.tensor_copy(gw[1][:], xw[1][:].indirect(offs_t[:]))
+        for t in range(PACK):
+            for h in range(2):
+                product(0, t, h)
+        deal("scalar", 1, w1b[0], 0, 64, 0)
+        deal("vector", 1, w1b[1], 64, 112, 64)
+        deal("scalar", 1, w1b[1], 112, 128, 64)
+        for t in range(PACK):
+            quant_w1(1, t, t + 1)
+            for h in range(2):
+                product(1, t, h)
+
+        w2b = sb([P, N * PACK], BF16, "w2b")
+        w2c = sb([P, N], U32, "w2c")
+        w2s = sb([P, N], U8, "w2s")
+        nc.vector.tensor_copy(
+            out=w2b[:].rearrange("p (c i t) -> p c t i", i=4, t=PACK),
+            in_=w2r[:].rearrange("p t (c i) -> p c t i", i=4),
+        )
+
+        y = [sb([P, S], F32, "y%d" % t) for t in range(PACK)]
+        hb = [sb([P, PACK, HALF], BF16, "hb%d" % h) for h in range(2)]
+
+        def evac(t, h, engine):
+            if engine == "scalar":
+                nc.scalar.activation(out=y[t][:, h * BANK : (h + 1) * BANK], in_=banks[t][h][:], func=ACT.Copy)
+            else:
+                nc.vector.tensor_copy(out=y[t][:, h * BANK : (h + 1) * BANK], in_=banks[t][h][:])
+
+        units = [[(0, 0), (0, 1)], [(1, 0), (1, 1)], [(2, 0), (3, 0)], [(2, 1), (3, 1)]]
+        sg = [sb([P, U], F32, "sg%d" % u) for u in range(4)]
+        sc = [sb([P, U], F32, "sc%d" % u) for u in range(4)]
+        pr = [sb([P, U // 2], F32, "pr%d" % u) for u in range(4)]
+        s4 = [sb([P, U // 4], F32, "s4%d" % u) for u in range(4)]
+        dv = [sb([P, U], F32, "dv%d" % u) for u in range(4)]
+        th = [sb([P, U], F32, "th%d" % u) for u in range(4)]
+        we = [sb([P, U], F32, "we%d" % u) for u in range(4)]
+
+        def fetch(u):
+            if u < 2:
+                nc.scalar.activation(out=sg[u][:], in_=y[u][:].indirect(got_t[:]), func=ACT.Copy)
+            else:
+                for k, (t, h) in enumerate(units[u]):
+                    nc.scalar.activation(out=sg[u][:, k * HALF : (k + 1) * HALF], in_=y[t][:].indirect(got_t[:, 16 * h : 16 * h + 16]), func=ACT.Copy)
+
+        def floor(u):
+            if u < 2:
+                nc.vector.tensor_tensor(out=sc[u][:], in0=sg[u][:], in1=fl[0][:, u, :], op=ALU.max)
+            else:
+                h = u - 2
+                nc.vector.tensor_tensor(
+                    out=sc[u][:].rearrange("p (k r) -> p k r", k=2),
+                    in0=sg[u][:].rearrange("p (k r) -> p k r", k=2),
+                    in1=fl[1][:, :, h * HALF : (h + 1) * HALF],
+                    op=ALU.max,
+                )
+
+        def pairs(u):
+            v = sc[u][:].rearrange("p (j a e) -> p j a e", a=2, e=2)
+            nc.vector.tensor_tensor(out=pr[u][:].rearrange("p (j e) -> p j e", e=2), in0=v[:, :, 0, :], in1=v[:, :, 1, :], op=ALU.add)
+
+        def sums(u):
+            v = pr[u][:].rearrange("p (j e) -> p j e", e=2)
+            nc.vector.tensor_tensor(out=s4[u][:], in0=v[:, :, 0], in1=v[:, :, 1], op=ALU.add)
+
+        def centre(u):
+            nc.vector.scalar_tensor_tensor(
+                out=dv[u][:].rearrange("p (j d) -> p j d", d=D),
+                in0=s4[u][:].unsqueeze(2).to_broadcast([P, U // D, D]),
+                scalar=-0.25,
+                in1=sc[u][:].rearrange("p (j d) -> p j d", d=D),
+                op0=ALU.mult,
+                op1=ALU.add,
+            )
+
+        def weigh(u):
+            nc.scalar.activation(out=th[u][:], in_=dv[u][:], func=ACT.Tanh)
+            nc.scalar.activation(out=we[u][:], in_=th[u][:], func=ACT.Exp, scale=1.2)
+
+        def hidden(u):
+            for k, (t, h) in enumerate(units[u]):
+                cols = slice(k * HALF, (k + 1) * HALF)
+                nc.vector.scalar_tensor_tensor(out=hb[h][:, t, :], in0=we[u][:, cols], scalar=un[:, t : t + 1], in1=sc[u][:, cols], op0=ALU.mult, op1=ALU.mult)
+
+        hq = [sb([P, HALF * PACK], BF16, "hq%d" % h) for h in range(2)]
+        hc = [sb([P, HALF], U32, "hc%d" % h) for h in range(2)]
+        hs = [sb([P, HALF], U8, "hs%d" % h) for h in range(2)]
+        res = [sb([P, HALF], F32, "res%d" % h) for h in range(2)]
+
+        def weave(h):
+            nc.vector.tensor_copy(
+                out=hq[h][:].rearrange("p (c i t) -> p c t i", i=4, t=PACK),
+                in_=hb[h][:].rearrange("p t (c i) -> p c t i", i=4),
+            )
+
+        def mix(h):
+            nc.vector.quantize_mx(out=hc[h][:].bitcast(FP8X4), scales=hs[h][:], in_=hq[h][:])
+            acc = psum.tile([P, BANK], F32, name="acc%d" % h, tag="bank0%d" % h)
+            nc.tensor.matmul_mx(out=acc[:, 0:HALF], lhsT=w2c[:].bitcast(FP8X4), lhsT_scale=w2s[:], rhs=hc[h][:].bitcast(FP8X4), rhs_scale=hs[h][:], start=True, stop=True)
+            nc.scalar.activation(out=res[h][:], in_=acc[:, 0:HALF], func=ACT.Copy)
+            nc.sync.dma_start(out=out[:, h * HALF : (h + 1) * HALF], in_=res[h][:])
+
+        evac(0, 0, "vector")
+        evac(0, 1, "scalar")
+        fetch(0)
+        nc.vector.quantize_mx(out=w2c[:].bitcast(FP8X4), scales=w2s[:], in_=w2b[:])
+        evac(1, 0, "vector")
+        evac(1, 1, "scalar")
+        fetch(1)
+        evac(2, 0, "vector")
+        floor(0)
+        evac(3, 0, "vector")
+        pairs(0)
+        sums(0)
+        centre(0)
+        weigh(0)
+        floor(1)
+        pairs(1)
+        sums(1)
+        centre(1)
+        evac(2, 1, "scalar")
+        evac(3, 1, "scalar")
+        fetch(2)
+        hidden(0)
+        weigh(1)
+        fetch(3)
+        floor(2)
+        pairs(2)
+        hidden(1)
+        sums(2)
+        centre(2)
+        weigh(2)
+        floor(3)
+        pairs(3)
+        sums(3)
+        centre(3)
+        weigh(3)
+        hidden(2)
+        weave(0)
+        hidden(3)
+        mix(0)
+        weave(1)
+        mix(1)

@@ -44,11 +44,11 @@ def tile_picked_yxtrim_soft_p_kernel(tc, x_words, x_scales, w1, flr, unit, w2, o
         def load_words(o):
             nc.sync.dma_start(out=xw[o][:].bitcast(I32), in_=x_words[o].rearrange("p n t -> p (n t)").bitcast(I32))
 
-        nc.vector.memset(xs[:].bitcast(I32), 0)
-        load_words(0)
+        nc.vector.memset(xs[32:64, :].bitcast(I32), 0)
+        nc.vector.memset(xs[64:128, :].bitcast(I32), 0)
+        nc.sync.dma_start(out=xs[0:32, :].bitcast(I32), in_=x_scales.rearrange("o q c -> (o q) c").bitcast(I32))
         nc.sync.dma_start(offs_t[:], offs)
-        for q in range(4):
-            nc.gpsimd.dma_start(out=xs[32 * q : 32 * q + 8, :].bitcast(I32), in_=x_scales[:, 4 * q : 4 * q + 4, :].bitcast(I32))
+        load_words(0)
         w1v = w1.rearrange("(o p j) c -> o p j c", o=2, j=PACK)
         nc.sync.dma_start(out=w1a[:], in_=w1v[0])
         load_words(1)
@@ -62,7 +62,10 @@ def tile_picked_yxtrim_soft_p_kernel(tc, x_words, x_scales, w1, flr, unit, w2, o
         nc.sync.dma_start(out=fl[1][:], in_=flv[:, 2:4, :])
 
         gw = [sb([P, S], U32, "gw%d" % o) for o in range(2)]
-        gs = sb([P, S], U8, "gs")
+        gs = [sb([P, S], U8, "gs%d" % o) for o in range(2)]
+        gs0 = sb([P, S], U8, "gflat")
+        for o in range(2):
+            nc.gpsimd.memset(gs[o][:].bitcast(I32), 0)
         wb = [sb([P, PACK * P * PACK], BF16, "wb%d" % o) for o in range(2)]
         wc = [sb([P, H], U32, "wc%d" % o) for o in range(2)]
         ws = [sb([P, H], U8, "ws%d" % o) for o in range(2)]
@@ -87,13 +90,16 @@ def tile_picked_yxtrim_soft_p_kernel(tc, x_words, x_scales, w1, flr, unit, w2, o
                 lhsT=wc[o][:, t * P : (t + 1) * P].bitcast(FP8X4),
                 lhsT_scale=ws[o][:, t * P : (t + 1) * P],
                 rhs=gw[o][:, cols].bitcast(FP8X4),
-                rhs_scale=gs[4 * o : P, cols],
+                rhs_scale=gs[o][:, cols],
                 start=(o == 0),
                 stop=(o == 1),
             )
 
+        nc.vector.tensor_copy(gs0[:], xs[:].indirect(offs_t[:]))
+        for o in range(2):
+            for q in range(4):
+                nc.gpsimd.dma_start(out=gs[o][32 * q : 32 * q + 4, :].bitcast(I32), in_=gs0[16 * o + 4 * q : 16 * o + 4 * q + 4, :].bitcast(I32))
         nc.vector.tensor_copy(gw[0][:], xw[0][:].indirect(offs_t[:]))
-        nc.vector.tensor_copy(gs[:], xs[:].indirect(offs_t[:]))
         deal("scalar", 0, w1a, 0, 128, 0)
         quant_w1(0, 0, 4)
         nc.vector.tensor_copy(gw[1][:], xw[1][:].indirect(offs_t[:]))
@@ -175,8 +181,9 @@ def tile_picked_yxtrim_soft_p_kernel(tc, x_words, x_scales, w1, flr, unit, w2, o
             nc.scalar.activation(out=th[u][:], in_=dv[u][:], func=ACT.Tanh)
             nc.scalar.activation(out=we[u][:], in_=th[u][:], func=ACT.Exp, scale=1.2)
 
-        def hidden(u):
-            for k, (t, h) in enumerate(units[u]):
+        def hidden(u, pieces=(0, 1)):
+            for k in pieces:
+                t, h = units[u][k]
                 cols = slice(k * HALF, (k + 1) * HALF)
                 nc.vector.scalar_tensor_tensor(out=hb[h][:, t, :], in0=we[u][:, cols], scalar=un[:, t : t + 1], in1=sc[u][:, cols], op0=ALU.mult, op1=ALU.mult)
 
@@ -186,56 +193,62 @@ def tile_picked_yxtrim_soft_p_kernel(tc, x_words, x_scales, w1, flr, unit, w2, o
         res = [sb([P, HALF], F32, "res%d" % h) for h in range(2)]
 
         def weave(h):
-            nc.vector.tensor_copy(
-                out=hq[h][:].rearrange("p (c i t) -> p c t i", i=4, t=PACK),
-                in_=hb[h][:].rearrange("p t (c i) -> p c t i", i=4),
-            )
+            dst = hq[h][:].rearrange("p (c i t) -> p c t i", i=4, t=PACK)
+            src = hb[h][:].rearrange("p t (c i) -> p c t i", i=4)
+            if h == 0:
+                nc.scalar.copy(out=dst, in_=src)
+            else:
+                nc.vector.tensor_copy(out=dst, in_=src)
 
         def mix(h):
             nc.vector.quantize_mx(out=hc[h][:].bitcast(FP8X4), scales=hs[h][:], in_=hq[h][:])
             acc = psum.tile([P, BANK], F32, name="acc%d" % h, tag="bank0%d" % h)
             nc.tensor.matmul_mx(out=acc[:, 0:HALF], lhsT=w2c[:].bitcast(FP8X4), lhsT_scale=w2s[:], rhs=hc[h][:].bitcast(FP8X4), rhs_scale=hs[h][:], start=True, stop=True)
-            nc.scalar.activation(out=res[h][:], in_=acc[:, 0:HALF], func=ACT.Copy)
+            if h == 1:
+                nc.scalar.activation(out=res[h][:], in_=acc[:, 0:HALF], func=ACT.Copy)
+            else:
+                nc.vector.tensor_copy(out=res[h][:], in_=acc[:, 0:HALF])
             nc.sync.dma_start(out=out[:, h * HALF : (h + 1) * HALF], in_=res[h][:])
 
+        nc.vector.quantize_mx(out=w2c[:].bitcast(FP8X4), scales=w2s[:], in_=w2b[:])
         evac(0, 0, "vector")
         evac(0, 1, "scalar")
         fetch(0)
-        nc.vector.quantize_mx(out=w2c[:].bitcast(FP8X4), scales=w2s[:], in_=w2b[:])
         evac(1, 0, "vector")
         evac(1, 1, "scalar")
         fetch(1)
         evac(2, 0, "vector")
+        evac(2, 1, "vector")
         floor(0)
         evac(3, 0, "vector")
         pairs(0)
+        evac(3, 1, "vector")
         sums(0)
+        fetch(2)
+        floor(1)
         centre(0)
         weigh(0)
-        floor(1)
-        pairs(1)
-        sums(1)
-        centre(1)
-        evac(2, 1, "scalar")
-        evac(3, 1, "scalar")
-        fetch(2)
-        hidden(0)
-        weigh(1)
         fetch(3)
+        pairs(1)
         floor(2)
+        sums(1)
         pairs(2)
-        hidden(1)
+        centre(1)
+        weigh(1)
         sums(2)
+        floor(3)
         centre(2)
         weigh(2)
-        floor(3)
         pairs(3)
+        hidden(0, (0,))
         sums(3)
+        hidden(0, (1,))
         centre(3)
         weigh(3)
+        hidden(1)
         hidden(2)
         weave(0)
         hidden(3)
-        mix(0)
         weave(1)
         mix(1)
+        mix(0)

@@ -26,60 +26,58 @@ def tile_picked_yxtrim_soft_p_kernel(tc, x_words, x_scales, w1, flr, unit, w2, o
     nc = tc.nc
     with ExitStack() as ctx:
         keep = ctx.enter_context(tc.tile_pool(name="keep", bufs=1))
+        reuse = ctx.enter_context(tc.tile_pool(name="reuse", bufs=1))
         psum = ctx.enter_context(tc.psum_pool(name="psum", bufs=1))
 
         def sb(shape, dtype, name):
             return keep.tile(shape, dtype, name=name, align_bytes=64)
 
+        def at(offset, shape, dtype, name):
+            return reuse.tile(shape, dtype, name=name, align_bytes=64, offset=offset)
+
         offs_t = keep.tile([P, S // 16], U16, name="offs_t")
         got_t = keep.tile([P, U // 16], U16, name="got_t")
-        xw = [sb([P, T], U32, "xw%d" % o) for o in range(2)]
-        xs = sb([P, T], U8, "xs")
+        KB = 1024
+        xw = [at(24 * KB, [P, T], U32, "xw0"), at(0, [P, T], U32, "xw1")]
+        xs = at(14 * KB, [P, T], U8, "xs")
         w1a = sb([P, PACK, H], F32, "w1a")
-        w1b = [sb([P, PACK, H // 2], F32, "w1b%d" % c) for c in range(2)]
-        w2r = sb([P, PACK, N], F32, "w2r")
-        fl = [sb([P, 2, U], F32, "fl%d" % c) for c in range(2)]
-        un = sb([P, PACK], F32, "un")
+        w1b = at(16 * KB, [P, PACK, H], F32, "w1b")
+        w2r = at(28 * KB, [P, PACK, N], F32, "w2r")
+        fl = [at((32 + 4 * c) * KB, [P, 2, U], F32, "fl%d" % c) for c in range(2)]
+        un = at(30 * KB, [P, PACK], F32, "un")
 
-        def load_words(o):
-            nc.sync.dma_start(out=xw[o][:].bitcast(I32), in_=x_words[o].rearrange("p n t -> p (n t)").bitcast(I32))
+        def load_words(o, c0, c1):
+            nc.sync.dma_start(out=xw[o][:, c0:c1].bitcast(I32), in_=x_words[o].rearrange("p n t -> p (n t)").bitcast(I32)[:, c0:c1])
 
         nc.vector.memset(xs[32:64, :].bitcast(I32), 0)
         nc.vector.memset(xs[64:128, :].bitcast(I32), 0)
         nc.sync.dma_start(out=xs[0:32, :].bitcast(I32), in_=x_scales.rearrange("o q c -> (o q) c").bitcast(I32))
         nc.sync.dma_start(offs_t[:], offs)
-        load_words(0)
+        load_words(0, 0, T)
+        nc.sync.dma_start(got_t[:], got)
         w1v = w1.rearrange("(o p j) c -> o p j c", o=2, j=PACK)
         nc.sync.dma_start(out=w1a[:], in_=w1v[0])
-        load_words(1)
-        for c in range(2):
-            nc.sync.dma_start(out=w1b[c][:], in_=w1v[1][:, :, c * 256 : (c + 1) * 256])
-        nc.sync.dma_start(out=w2r[:], in_=w2.rearrange("(p t) m -> p t m", t=PACK))
-        nc.sync.dma_start(got_t[:], got)
-        flv = flr.rearrange("(p t) r -> p t r", t=PACK)
-        nc.sync.dma_start(out=fl[0][:], in_=flv[:, 0:2, :])
-        nc.sync.dma_start(out=un[:], in_=unit.rearrange("(p t) one -> p (t one)", t=PACK))
-        nc.sync.dma_start(out=fl[1][:], in_=flv[:, 2:4, :])
 
         gw = [sb([P, S], U32, "gw%d" % o) for o in range(2)]
         gs = [sb([P, S], U8, "gs%d" % o) for o in range(2)]
         gs0 = sb([P, S], U8, "gflat")
         for o in range(2):
             nc.gpsimd.memset(gs[o][:].bitcast(I32), 0)
-        wb = [sb([P, PACK * P * PACK], BF16, "wb%d" % o) for o in range(2)]
+        wb = [[sb([P, 2 * P * PACK], BF16, "wb%d%d" % (o, tp)) for tp in range(2)] for o in range(2)]
         wc = [sb([P, H], U32, "wc%d" % o) for o in range(2)]
         ws = [sb([P, H], U8, "ws%d" % o) for o in range(2)]
 
-        def deal(engine, o, raw, m0, m1, base):
-            dst = wb[o][:].rearrange("p (t m j) -> p m j t", t=PACK, j=PACK)[:, m0:m1]
-            src = raw[:].rearrange("p j (m t) -> p m j t", t=PACK)[:, m0 - base : m1 - base]
+        def deal(engine, o, raw, tp, m0, m1):
+            dst = wb[o][tp][:].rearrange("p (e m j) -> p m j e", e=2, j=PACK)[:, m0:m1]
+            src = raw[:].rearrange("p j (m tp e) -> p tp m j e", tp=2, e=2)[:, tp, m0:m1]
             if engine == "scalar":
                 nc.scalar.activation(out=dst, in_=src, func=ACT.Copy)
             else:
                 nc.vector.tensor_copy(out=dst, in_=src)
 
         def quant_w1(o, t0, t1):
-            nc.vector.quantize_mx(out=wc[o][:, t0 * P : t1 * P].bitcast(FP8X4), scales=ws[o][:, t0 * P : t1 * P], in_=wb[o][:, t0 * 512 : t1 * 512])
+            e0, e1 = t0 % 2, (t1 - 1) % 2 + 1
+            nc.vector.quantize_mx(out=wc[o][:, t0 * P : t1 * P].bitcast(FP8X4), scales=ws[o][:, t0 * P : t1 * P], in_=wb[o][t0 // 2][:, e0 * 512 : e1 * 512])
 
         banks = [[psum.tile([P, BANK], F32, name="bank%d%d" % (t, h), tag="bank%d%d" % (t, h)) for h in range(2)] for t in range(PACK)]
 
@@ -95,35 +93,48 @@ def tile_picked_yxtrim_soft_p_kernel(tc, x_words, x_scales, w1, flr, unit, w2, o
                 stop=(o == 1),
             )
 
-        nc.vector.tensor_copy(gs0[:], xs[:].indirect(offs_t[:]))
-        for o in range(2):
+        def place(o):
             for q in range(4):
-                nc.gpsimd.dma_start(out=gs[o][32 * q : 32 * q + 4, :].bitcast(I32), in_=gs0[16 * o + 4 * q : 16 * o + 4 * q + 4, :].bitcast(I32))
+                nc.sync.dma_start(out=gs[o][32 * q : 32 * q + 4, :].bitcast(I32), in_=gs0[16 * o + 4 * q : 16 * o + 4 * q + 4, :].bitcast(I32))
+
+        nc.vector.tensor_copy(gs0[:], xs[:].indirect(offs_t[:]))
+        load_words(1, 0, 3072)
+        place(0)
+        load_words(1, 3072, T)
+        nc.sync.dma_start(out=w1b[:], in_=w1v[1])
+        place(1)
         nc.vector.tensor_copy(gw[0][:], xw[0][:].indirect(offs_t[:]))
-        deal("scalar", 0, w1a, 0, 128, 0)
-        quant_w1(0, 0, 4)
+        nc.sync.dma_start(out=w2r[:], in_=w2.rearrange("(p t) m -> p t m", t=PACK))
+        nc.sync.dma_start(out=un[:], in_=unit.rearrange("(p t) one -> p (t one)", t=PACK))
+        flv = flr.rearrange("(p t) r -> p t r", t=PACK)
+        for c in range(2):
+            nc.sync.dma_start(out=fl[c][:], in_=flv[:, 2 * c : 2 * c + 2, :])
+        for tp in range(2):
+            deal("scalar", 0, w1a, tp, 0, 128)
+            quant_w1(0, 2 * tp, 2 * tp + 2)
         nc.vector.tensor_copy(gw[1][:], xw[1][:].indirect(offs_t[:]))
         for t in range(PACK):
             for h in range(2):
                 product(0, t, h)
-        deal("scalar", 1, w1b[0], 0, 64, 0)
-        deal("vector", 1, w1b[1], 64, 112, 64)
-        deal("scalar", 1, w1b[1], 112, 128, 64)
-        for t in range(PACK):
-            quant_w1(1, t, t + 1)
-            for h in range(2):
-                product(1, t, h)
+        for tp, split in ((0, 80), (1, 48)):
+            deal("vector", 1, w1b, tp, 0, split)
+            deal("scalar", 1, w1b, tp, split, P)
+            for t0, t1 in ((0, 1), (1, 2)) if tp == 0 else ((2, 4),):
+                quant_w1(1, t0, t1)
+                for t in range(t0, t1):
+                    for h in range(2):
+                        product(1, t, h)
 
         w2b = sb([P, N * PACK], BF16, "w2b")
         w2c = sb([P, N], U32, "w2c")
         w2s = sb([P, N], U8, "w2s")
-        nc.vector.tensor_copy(
+        nc.scalar.copy(
             out=w2b[:].rearrange("p (c i t) -> p c t i", i=4, t=PACK),
             in_=w2r[:].rearrange("p t (c i) -> p c t i", i=4),
         )
 
         y = [sb([P, S], F32, "y%d" % t) for t in range(PACK)]
-        hb = [sb([P, PACK, HALF], BF16, "hb%d" % h) for h in range(2)]
+        hb = sb([P, 2, PACK, HALF], BF16, "hb")
 
         def evac(t, h, engine):
             if engine == "scalar":
@@ -131,33 +142,27 @@ def tile_picked_yxtrim_soft_p_kernel(tc, x_words, x_scales, w1, flr, unit, w2, o
             else:
                 nc.vector.tensor_copy(out=y[t][:, h * BANK : (h + 1) * BANK], in_=banks[t][h][:])
 
-        units = [[(0, 0), (0, 1)], [(1, 0), (1, 1)], [(2, 0), (3, 0)], [(2, 1), (3, 1)]]
-        sg = [sb([P, U], F32, "sg%d" % u) for u in range(4)]
-        sc = [sb([P, U], F32, "sc%d" % u) for u in range(4)]
-        pr = [sb([P, U // 2], F32, "pr%d" % u) for u in range(4)]
-        s4 = [sb([P, U // 4], F32, "s4%d" % u) for u in range(4)]
-        dv = [sb([P, U], F32, "dv%d" % u) for u in range(4)]
-        th = [sb([P, U], F32, "th%d" % u) for u in range(4)]
-        we = [sb([P, U], F32, "we%d" % u) for u in range(4)]
+        units = [(0, 0, U), (1, 0, U), (2, 0, U), (3, 0, HALF), (3, HALF, U)]
+        wid = [r1 - r0 for t, r0, r1 in units]
+        sg = [sb([P, w], F32, "sg%d" % u) for u, w in enumerate(wid)]
+        sc = [sb([P, w], F32, "sc%d" % u) for u, w in enumerate(wid)]
+        pr = [sb([P, w // 2], F32, "pr%d" % u) for u, w in enumerate(wid)]
+        s4 = [sb([P, w // 4], F32, "s4%d" % u) for u, w in enumerate(wid)]
+        dv = [sb([P, w], F32, "dv%d" % u) for u, w in enumerate(wid)]
+        th = [sb([P, w], F32, "th%d" % u) for u, w in enumerate(wid)]
+        we = [sb([P, w], F32, "we%d" % u) for u, w in enumerate(wid)]
 
-        def fetch(u):
-            if u < 2:
-                nc.scalar.activation(out=sg[u][:], in_=y[u][:].indirect(got_t[:]), func=ACT.Copy)
+        def fetch(u, engine):
+            t, r0, r1 = units[u]
+            src = y[t][:].indirect(got_t[:, r0 // 16 : r1 // 16])
+            if engine == "scalar":
+                nc.scalar.activation(out=sg[u][:], in_=src, func=ACT.Copy)
             else:
-                for k, (t, h) in enumerate(units[u]):
-                    nc.scalar.activation(out=sg[u][:, k * HALF : (k + 1) * HALF], in_=y[t][:].indirect(got_t[:, 16 * h : 16 * h + 16]), func=ACT.Copy)
+                nc.vector.tensor_copy(out=sg[u][:], in_=src)
 
         def floor(u):
-            if u < 2:
-                nc.vector.tensor_tensor(out=sc[u][:], in0=sg[u][:], in1=fl[0][:, u, :], op=ALU.max)
-            else:
-                h = u - 2
-                nc.vector.tensor_tensor(
-                    out=sc[u][:].rearrange("p (k r) -> p k r", k=2),
-                    in0=sg[u][:].rearrange("p (k r) -> p k r", k=2),
-                    in1=fl[1][:, :, h * HALF : (h + 1) * HALF],
-                    op=ALU.max,
-                )
+            t, r0, r1 = units[u]
+            nc.vector.tensor_tensor(out=sc[u][:], in0=sg[u][:], in1=fl[t // 2][:, t % 2, r0:r1], op=ALU.max)
 
         def pairs(u):
             v = sc[u][:].rearrange("p (j a e) -> p j a e", a=2, e=2)
@@ -170,22 +175,29 @@ def tile_picked_yxtrim_soft_p_kernel(tc, x_words, x_scales, w1, flr, unit, w2, o
         def centre(u):
             nc.vector.scalar_tensor_tensor(
                 out=dv[u][:].rearrange("p (j d) -> p j d", d=D),
-                in0=s4[u][:].unsqueeze(2).to_broadcast([P, U // D, D]),
+                in0=s4[u][:].unsqueeze(2).to_broadcast([P, wid[u] // D, D]),
                 scalar=-0.25,
                 in1=sc[u][:].rearrange("p (j d) -> p j d", d=D),
                 op0=ALU.mult,
                 op1=ALU.add,
             )
 
-        def weigh(u):
+        def bend(u):
             nc.scalar.activation(out=th[u][:], in_=dv[u][:], func=ACT.Tanh)
+
+        def weigh(u):
             nc.scalar.activation(out=we[u][:], in_=th[u][:], func=ACT.Exp, scale=1.2)
 
-        def hidden(u, pieces=(0, 1)):
-            for k in pieces:
-                t, h = units[u][k]
-                cols = slice(k * HALF, (k + 1) * HALF)
-                nc.vector.scalar_tensor_tensor(out=hb[h][:, t, :], in0=we[u][:, cols], scalar=un[:, t : t + 1], in1=sc[u][:, cols], op0=ALU.mult, op1=ALU.mult)
+        def hidden(u):
+            t, r0, r1 = units[u]
+            nc.vector.scalar_tensor_tensor(
+                out=hb[:, r0 // HALF : r1 // HALF, t, :],
+                in0=we[u][:].rearrange("p (h r) -> p h r", r=HALF),
+                scalar=un[:, t : t + 1],
+                in1=sc[u][:].rearrange("p (h r) -> p h r", r=HALF),
+                op0=ALU.mult,
+                op1=ALU.mult,
+            )
 
         hq = [sb([P, HALF * PACK], BF16, "hq%d" % h) for h in range(2)]
         hc = [sb([P, HALF], U32, "hc%d" % h) for h in range(2)]
@@ -194,17 +206,15 @@ def tile_picked_yxtrim_soft_p_kernel(tc, x_words, x_scales, w1, flr, unit, w2, o
 
         def weave(h):
             dst = hq[h][:].rearrange("p (c i t) -> p c t i", i=4, t=PACK)
-            src = hb[h][:].rearrange("p t (c i) -> p c t i", i=4)
-            if h == 0:
-                nc.scalar.copy(out=dst, in_=src)
-            else:
-                nc.vector.tensor_copy(out=dst, in_=src)
+            src = hb[:, h].rearrange("p t (c i) -> p c t i", i=4)
+            nc.vector.tensor_copy(out=dst[:, 0:32], in_=src[:, 0:32])
+            nc.scalar.copy(out=dst[:, 32:64], in_=src[:, 32:64])
 
         def mix(h):
             nc.vector.quantize_mx(out=hc[h][:].bitcast(FP8X4), scales=hs[h][:], in_=hq[h][:])
             acc = psum.tile([P, BANK], F32, name="acc%d" % h, tag="bank0%d" % h)
             nc.tensor.matmul_mx(out=acc[:, 0:HALF], lhsT=w2c[:].bitcast(FP8X4), lhsT_scale=w2s[:], rhs=hc[h][:].bitcast(FP8X4), rhs_scale=hs[h][:], start=True, stop=True)
-            if h == 1:
+            if h == 0:
                 nc.scalar.activation(out=res[h][:], in_=acc[:, 0:HALF], func=ACT.Copy)
             else:
                 nc.vector.tensor_copy(out=res[h][:], in_=acc[:, 0:HALF])
@@ -213,42 +223,39 @@ def tile_picked_yxtrim_soft_p_kernel(tc, x_words, x_scales, w1, flr, unit, w2, o
         nc.vector.quantize_mx(out=w2c[:].bitcast(FP8X4), scales=w2s[:], in_=w2b[:])
         evac(0, 0, "vector")
         evac(0, 1, "scalar")
-        fetch(0)
         evac(1, 0, "vector")
         evac(1, 1, "scalar")
-        fetch(1)
+        fetch(0, "scalar")
         evac(2, 0, "vector")
-        evac(2, 1, "vector")
-        floor(0)
-        evac(3, 0, "vector")
-        pairs(0)
-        evac(3, 1, "vector")
-        sums(0)
-        fetch(2)
-        floor(1)
-        centre(0)
-        weigh(0)
-        fetch(3)
-        pairs(1)
-        floor(2)
-        sums(1)
-        pairs(2)
-        centre(1)
-        weigh(1)
-        sums(2)
-        floor(3)
+        fetch(1, "vector")
+        evac(2, 1, "scalar")
+        evac(3, 0, "scalar")
+        evac(3, 1, "scalar")
+        for u in (2, 3, 4):
+            fetch(u, "scalar")
+        for stage in (floor, pairs, sums, centre, bend, weigh):
+            stage(0)
+            stage(1)
+        for stage in (floor, pairs, sums):
+            stage(2)
+            stage(3)
+        floor(4)
         centre(2)
-        weigh(2)
-        pairs(3)
-        hidden(0, (0,))
-        sums(3)
-        hidden(0, (1,))
+        pairs(4)
         centre(3)
-        weigh(3)
+        sums(4)
+        hidden(0)
+        centre(4)
         hidden(1)
+        for stage in (bend, weigh):
+            stage(2)
+            stage(3)
+        bend(4)
+        weigh(4)
         hidden(2)
-        weave(0)
         hidden(3)
+        weave(0)
+        hidden(4)
         weave(1)
-        mix(1)
         mix(0)
+        mix(1)

from contextlib import ExitStack

import concourse.mybir as mybir

K, T, S, D, N, H, U = 1024, 4096, 1024, 4, 128, 512, 512
FLOPS = 2 * K * H * S + 2 * H * N * U

F32 = mybir.dt.float32
BF16 = mybir.dt.bfloat16
I32 = mybir.dt.int32
U32 = mybir.dt.uint32
U16 = mybir.dt.uint16
U8 = mybir.dt.uint8
FP8X4 = mybir.dt.float8_e4m3fn_x4
ALU = mybir.AluOpType
ACT = mybir.ActivationFunctionType
AX = mybir.AxisListType

P = 128
PACK = 4
BANK = 512
HALF = U // 2


def tile_picked_yxtrim_soft_p_kernel(tc, x_words, x_scales, w1, flr, unit, w2, offs, got, out):
    nc = tc.nc
    with ExitStack() as ctx:
        keep = ctx.enter_context(tc.tile_pool(name="keep", bufs=1))
        reuse = ctx.enter_context(tc.tile_pool(name="reuse", bufs=1))
        psum = ctx.enter_context(tc.psum_pool(name="psum", bufs=1))

        def sb(shape, dtype, name):
            return keep.tile(shape, dtype, name=name, align_bytes=64)

        def at(offset, shape, dtype, name):
            return reuse.tile(shape, dtype, name=name, align_bytes=64, offset=offset)

        offs_t = keep.tile([P, S // 16], U16, name="offs_t")
        got_t = keep.tile([P, U // 16], U16, name="got_t")
        KB = 1024
        xw = [at(24 * KB, [P, T], U32, "xw0"), at(0, [P, T], U32, "xw1")]
        xs = at(14 * KB, [P, T], U8, "xs")
        w1a = sb([P, PACK, H], F32, "w1a")
        w1b = at(16 * KB, [P, PACK, H], F32, "w1b")
        w2r = at(28 * KB, [P, PACK, N], F32, "w2r")
        fl = [at((32 + 4 * c) * KB, [P, 2, U], F32, "fl%d" % c) for c in range(2)]
        un = at(30 * KB, [P, PACK], F32, "un")

        def load_words(o, c0, c1):
            nc.sync.dma_start(out=xw[o][:, c0:c1].bitcast(I32), in_=x_words[o].rearrange("p n t -> p (n t)").bitcast(I32)[:, c0:c1])

        nc.vector.memset(xs[32:64, :].bitcast(I32), 0)
        nc.vector.memset(xs[64:128, :].bitcast(I32), 0)
        nc.sync.dma_start(out=xs[0:32, :].bitcast(I32), in_=x_scales.rearrange("o q c -> (o q) c").bitcast(I32))
        nc.sync.dma_start(offs_t[:], offs)
        load_words(0, 0, T)
        nc.sync.dma_start(got_t[:], got)
        w1v = w1.rearrange("(o p j) c -> o p j c", o=2, j=PACK)
        nc.sync.dma_start(out=w1a[:], in_=w1v[0])

        gw = [sb([P, S], U32, "gw%d" % o) for o in range(2)]
        gs = [sb([P, S], U8, "gs%d" % o) for o in range(2)]
        gs0 = sb([P, S], U8, "gflat")
        for o in range(2):
            nc.gpsimd.memset(gs[o][:].bitcast(I32), 0)
        wb = [[sb([P, 2 * P * PACK], BF16, "wb%d%d" % (o, tp)) for tp in range(2)] for o in range(2)]
        wc = [sb([P, H], U32, "wc%d" % o) for o in range(2)]
        ws = [sb([P, H], U8, "ws%d" % o) for o in range(2)]

        def deal(engine, o, raw, tp, m0, m1):
            dst = wb[o][tp][:].rearrange("p (e m j) -> p m j e", e=2, j=PACK)[:, m0:m1]
            src = raw[:].rearrange("p j (m tp e) -> p tp m j e", tp=2, e=2)[:, tp, m0:m1]
            if engine == "scalar":
                nc.scalar.activation(out=dst, in_=src, func=ACT.Copy)
            else:
                nc.vector.tensor_copy(out=dst, in_=src)

        def quant_w1(o, t0, t1):
            e0, e1 = t0 % 2, (t1 - 1) % 2 + 1
            nc.vector.quantize_mx(out=wc[o][:, t0 * P : t1 * P].bitcast(FP8X4), scales=ws[o][:, t0 * P : t1 * P], in_=wb[o][t0 // 2][:, e0 * 512 : e1 * 512])

        banks = [[psum.tile([P, BANK], F32, name="bank%d%d" % (t, h), tag="bank%d%d" % (t, h)) for h in range(2)] for t in range(PACK)]

        def product(o, t, h):
            cols = slice(h * BANK, (h + 1) * BANK)
            nc.tensor.matmul_mx(
                out=banks[t][h][:],
                lhsT=wc[o][:, t * P : (t + 1) * P].bitcast(FP8X4),
                lhsT_scale=ws[o][:, t * P : (t + 1) * P],
                rhs=gw[o][:, cols].bitcast(FP8X4),
                rhs_scale=gs[o][:, cols],
                start=(o == 0),
                stop=(o == 1),
            )

        def place(o):
            for q in range(4):
                nc.sync.dma_start(out=gs[o][32 * q : 32 * q + 4, :].bitcast(I32), in_=gs0[16 * o + 4 * q : 16 * o + 4 * q + 4, :].bitcast(I32))

        nc.vector.tensor_copy(gs0[:], xs[:].indirect(offs_t[:]))
        load_words(1, 0, 3072)
        place(0)
        load_words(1, 3072, T)
        nc.sync.dma_start(out=w1b[:], in_=w1v[1])
        place(1)
        nc.vector.tensor_copy(gw[0][:], xw[0][:].indirect(offs_t[:]))
        nc.sync.dma_start(out=w2r[:], in_=w2.rearrange("(p t) m -> p t m", t=PACK))
        nc.sync.dma_start(out=un[:], in_=unit.rearrange("(p t) one -> p (t one)", t=PACK))
        flv = flr.rearrange("(p t) r -> p t r", t=PACK)
        for c in range(2):
            nc.sync.dma_start(out=fl[c][:], in_=flv[:, 2 * c : 2 * c + 2, :])
        for tp in range(2):
            deal("scalar", 0, w1a, tp, 0, 128)
            quant_w1(0, 2 * tp, 2 * tp + 2)
        nc.vector.tensor_copy(gw[1][:], xw[1][:].indirect(offs_t[:]))
        for t in range(PACK):
            for h in range(2):
                product(0, t, h)
        for tp, split in ((0, 80), (1, 48)):
            deal("vector", 1, w1b, tp, 0, split)
            deal("scalar", 1, w1b, tp, split, P)
            for t0, t1 in ((0, 1), (1, 2)) if tp == 0 else ((2, 4),):
                quant_w1(1, t0, t1)
                for t in range(t0, t1):
                    for h in range(2):
                        product(1, t, h)

        w2b = sb([P, N * PACK], BF16, "w2b")
        w2c = sb([P, N], U32, "w2c")
        w2s = sb([P, N], U8, "w2s")
        nc.scalar.copy(
            out=w2b[:].rearrange("p (c i t) -> p c t i", i=4, t=PACK),
            in_=w2r[:].rearrange("p t (c i) -> p c t i", i=4),
        )

        y = [sb([P, S], F32, "y%d" % t) for t in range(PACK)]
        hb = sb([P, 2, PACK, HALF], BF16, "hb")

        def evac(t, h, engine):
            if engine == "scalar":
                nc.scalar.activation(out=y[t][:, h * BANK : (h + 1) * BANK], in_=banks[t][h][:], func=ACT.Copy)
            else:
                nc.vector.tensor_copy(out=y[t][:, h * BANK : (h + 1) * BANK], in_=banks[t][h][:])

        units = [(0, 0, U), (1, 0, U), (2, 0, U), (3, 0, HALF), (3, HALF, U)]
        wid = [r1 - r0 for t, r0, r1 in units]
        sg = [sb([P, w], F32, "sg%d" % u) for u, w in enumerate(wid)]
        sc = [sb([P, w], F32, "sc%d" % u) for u, w in enumerate(wid)]
        pr = [sb([P, w // 2], F32, "pr%d" % u) for u, w in enumerate(wid)]
        s4 = [sb([P, w // 4], F32, "s4%d" % u) for u, w in enumerate(wid)]
        dv = [sb([P, w], F32, "dv%d" % u) for u, w in enumerate(wid)]
        th = [sb([P, w], F32, "th%d" % u) for u, w in enumerate(wid)]
        we = [sb([P, w], F32, "we%d" % u) for u, w in enumerate(wid)]

        def fetch(u, engine):
            t, r0, r1 = units[u]
            src = y[t][:].indirect(got_t[:, r0 // 16 : r1 // 16])
            if engine == "scalar":
                nc.scalar.activation(out=sg[u][:], in_=src, func=ACT.Copy)
            else:
                nc.vector.tensor_copy(out=sg[u][:], in_=src)

        def floor(u):
            t, r0, r1 = units[u]
            nc.vector.tensor_tensor(out=sc[u][:], in0=sg[u][:], in1=fl[t // 2][:, t % 2, r0:r1], op=ALU.max)

        def pairs(u):
            v = sc[u][:].rearrange("p (j a e) -> p j a e", a=2, e=2)
            nc.vector.tensor_tensor(out=pr[u][:].rearrange("p (j e) -> p j e", e=2), in0=v[:, :, 0, :], in1=v[:, :, 1, :], op=ALU.add)

        def sums(u):
            v = pr[u][:].rearrange("p (j e) -> p j e", e=2)
            nc.vector.tensor_tensor(out=s4[u][:], in0=v[:, :, 0], in1=v[:, :, 1], op=ALU.add)

        def centre(u):
            nc.vector.scalar_tensor_tensor(
                out=dv[u][:].rearrange("p (j d) -> p j d", d=D),
                in0=s4[u][:].unsqueeze(2).to_broadcast([P, wid[u] // D, D]),
                scalar=-0.25,
                in1=sc[u][:].rearrange("p (j d) -> p j d", d=D),
                op0=ALU.mult,
                op1=ALU.add,
            )

        def bend(u):
            nc.scalar.activation(out=th[u][:], in_=dv[u][:], func=ACT.Tanh)

        def weigh(u):
            nc.scalar.activation(out=we[u][:], in_=th[u][:], func=ACT.Exp, scale=1.2)

        def hidden(u):
            t, r0, r1 = units[u]
            nc.vector.scalar_tensor_tensor(
                out=hb[:, r0 // HALF : r1 // HALF, t, :],
                in0=we[u][:].rearrange("p (h r) -> p h r", r=HALF),
                scalar=un[:, t : t + 1],
                in1=sc[u][:].rearrange("p (h r) -> p h r", r=HALF),
                op0=ALU.mult,
                op1=ALU.mult,
            )

        hq = [sb([P, HALF * PACK], BF16, "hq%d" % h) for h in range(2)]
        hc = [sb([P, HALF], U32, "hc%d" % h) for h in range(2)]
        hs = [sb([P, HALF], U8, "hs%d" % h) for h in range(2)]
        res = [sb([P, HALF], F32, "res%d" % h) for h in range(2)]

        def weave(h):
            dst = hq[h][:].rearrange("p (c i t) -> p c t i", i=4, t=PACK)
            src = hb[:, h].rearrange("p t (c i) -> p c t i", i=4)
            nc.vector.tensor_copy(out=dst[:, 0:32], in_=src[:, 0:32])
            nc.scalar.copy(out=dst[:, 32:64], in_=src[:, 32:64])

        def mix(h):
            nc.vector.quantize_mx(out=hc[h][:].bitcast(FP8X4), scales=hs[h][:], in_=hq[h][:])
            acc = psum.tile([P, BANK], F32, name="acc%d" % h, tag="bank0%d" % h)
            nc.tensor.matmul_mx(out=acc[:, 0:HALF], lhsT=w2c[:].bitcast(FP8X4), lhsT_scale=w2s[:], rhs=hc[h][:].bitcast(FP8X4), rhs_scale=hs[h][:], start=True, stop=True)
            if h == 0:
                nc.scalar.activation(out=res[h][:], in_=acc[:, 0:HALF], func=ACT.Copy)
            else:
                nc.vector.tensor_copy(out=res[h][:], in_=acc[:, 0:HALF])
            nc.sync.dma_start(out=out[:, h * HALF : (h + 1) * HALF], in_=res[h][:])

        nc.vector.quantize_mx(out=w2c[:].bitcast(FP8X4), scales=w2s[:], in_=w2b[:])
        evac(0, 0, "vector")
        evac(0, 1, "scalar")
        evac(1, 0, "vector")
        evac(1, 1, "scalar")
        fetch(0, "scalar")
        evac(2, 0, "vector")
        fetch(1, "vector")
        evac(2, 1, "scalar")
        evac(3, 0, "scalar")
        evac(3, 1, "scalar")
        for u in (2, 3, 4):
            fetch(u, "scalar")
        for stage in (floor, pairs, sums, centre, bend, weigh):
            stage(0)
            stage(1)
        for stage in (floor, pairs, sums):
            stage(2)
            stage(3)
        floor(4)
        centre(2)
        pairs(4)
        centre(3)
        sums(4)
        hidden(0)
        centre(4)
        hidden(1)
        for stage in (bend, weigh):
            stage(2)
            stage(3)
        bend(4)
        weigh(4)
        hidden(2)
        hidden(3)
        weave(0)
        hidden(4)
        weave(1)
        mix(0)
        mix(1)
